import numpy as np
import ml_dtypes


def mxq(x, axis, fmt="e4m3"):
    dtype, down = {"e4m3": (ml_dtypes.float8_e4m3fn, 7), "e5m2": (ml_dtypes.float8_e5m2, 14)}[fmt]
    v = np.moveaxis(np.asarray(x, np.float32).astype(ml_dtypes.bfloat16).astype(np.float64), axis, -1)
    blocks = v.reshape(v.shape[:-1] + (-1, 32))
    amax = np.abs(blocks).max(-1, keepdims=True)
    byte = np.maximum(np.where(amax > 0, np.frexp(amax)[1] - 1 + 127, 0) - down, 1)
    scale = np.exp2(byte - 127.0)
    codes = (blocks / scale).astype(np.float32).astype(dtype).astype(np.float64)
    return np.moveaxis((codes * scale).reshape(v.shape), -1, axis)


WIDE = False


def mx_kscale(k):
    if not WIDE:
        return np.ones(k)
    levels = np.array([10, -10, 5, -5, 0])
    if k % 512:
        return np.exp2(np.random.permutation(np.resize(levels, k // 32))).repeat(32)
    a = np.empty((k // 512, 16))
    for p in range(k // 512):
        a[p, :8] = np.random.permutation(np.resize(levels, 8))
        for g in range(8):
            far = levels[np.abs(levels - a[p, g]) >= 10]
            a[p, g + 8] = far[np.random.randint(len(far))]
    return np.exp2(a.ravel()).repeat(32)


BF16 = ml_dtypes.bfloat16


def bf(x):
    return np.asarray(x, np.float32).astype(BF16)


def f64(x):
    return np.asarray(x).astype(np.float64)


E2M1 = np.array([0.0, 0.5, 1.0, 1.5, 2.0, 3.0, 4.0, 6.0, -0.0, -0.5, -1.0, -1.5, -2.0, -3.0, -4.0, -6.0])


def pack_weight(w, fmt):
    k, n = w.shape
    w = f64(bf(w)).reshape(k // 32, 32, n)
    amax = np.abs(w).max(1)
    if fmt == "e4m3":
        byte = np.frexp(amax)[1] - 1 + 127 - 7
    else:
        mant, ex = np.frexp(amax / 6.0)
        byte = np.where(mant > 0.5, ex, ex - 1) + 127
    byte = np.clip(np.where(amax > 0, byte, 1), 1, 254)
    scaled = (w * np.exp2(127.0 - byte)[:, None, :]).reshape(k, n).astype(np.float32)
    by_word = np.ascontiguousarray(scaled.reshape(k // 512, 128, 4, n).transpose(0, 1, 3, 2))
    if fmt == "e4m3":
        words = by_word.astype(ml_dtypes.float8_e4m3fn).view(np.uint8)
    else:
        c = by_word.astype(ml_dtypes.float4_e2m1fn).view(np.uint8) & 0xF
        words = c[..., 0::2] | (c[..., 1::2] << 4)
    return np.ascontiguousarray(words), np.ascontiguousarray(byte.astype(np.uint8).reshape(k // 512, 16, n))


def unpack_weight(words, scales, fmt):
    g, p, n, _ = words.shape
    if fmt == "e4m3":
        vals = np.ascontiguousarray(words).view(ml_dtypes.float8_e4m3fn).astype(np.float64)
    else:
        nib = np.empty((g, p, n, 4), np.uint8)
        nib[..., 0::2] = words & 0xF
        nib[..., 1::2] = words >> 4
        vals = E2M1[nib]
    vals = vals * np.repeat(np.exp2(scales.astype(np.float64) - 127.0), 8, axis=1)[..., None]
    return vals.transpose(0, 1, 3, 2).reshape(g * 512, n)
def pack4(w):
    words, scales = pack_weight(w, "e2m1")
    return words.reshape(words.shape[0], 128, -1), scales


def unpack4(words, scales):
    return unpack_weight(words.reshape(words.shape[0], 128, -1, 2), scales, "e2m1")


def planes(Y):
    n, m = Y.shape
    b = f64(bf(Y)).reshape(n // 32, 32, m)
    amax = np.abs(b).max(1)
    byte = np.clip(np.where(amax > 0, np.frexp(amax)[1] - 1 + 127 - 7, 1), 1, 254)
    codes = (b * np.exp2(127.0 - byte)[:, None, :]).reshape(n, m).astype(np.float32).astype(ml_dtypes.float8_e4m3fn).view(np.uint8)
    words = codes.reshape(n // 512, 128, 4, m).transpose(0, 1, 3, 2)
    return np.ascontiguousarray(words), np.ascontiguousarray(byte.astype(np.uint8).reshape(n // 512, 16, m))


T, K, N = 768, 1536, 1024

C_SPREAD = 0.5
R_SPREAD = 0.3
J_SPREAD = 0.8


def setup_inputs():
    s = mx_kscale(K)[:, None]
    own = np.exp(J_SPREAD * np.random.randn(N))[None, :]
    x_words, x_scales = pack_weight(np.random.randn(K, T) * s, "e4m3")
    a_words, a_scales = pack4(C_SPREAD * np.random.randn(K, N) / np.sqrt(K) / s)
    b_words, b_scales = pack_weight(np.random.randn(K, N) * own / np.sqrt(K) / s, "e4m3")
    d = bf(np.random.randn(K, N) * own / np.sqrt(K) / s)
    r = bf(np.exp(R_SPREAD * np.random.randn(T)))
    return {"x_words": x_words, "x_scales": x_scales, "a_words": a_words, "a_scales": a_scales,
            "b_words": b_words, "b_scales": b_scales, "d": d, "r": r}


def reference(x_words, x_scales, a_words, a_scales, b_words, b_scales, d, r):
    X = unpack_weight(x_words, x_scales, "e4m3")
    A = unpack4(a_words, a_scales)
    B = unpack_weight(b_words, b_scales, "e4m3")
    cross = X.T @ A
    pos = X.T @ B
    rest = X.T @ mxq(f64(d), 0, "e4m3")
    weight = np.exp(cross) * f64(r)[:, None]
    y = weight * pos + rest
    Y = y.T
    words, scales = planes(Y)
    return y, words, scales

@@ -1,0 +1,349 @@
+from contextlib import ExitStack
+
+import concourse.mybir as mybir
+from concourse.masks import make_identity
+
+T, K, N = 768, 1536, 1024
+FLOPS = 3 * 2 * T * K * N
+
+F32 = mybir.dt.float32
+BF16 = mybir.dt.bfloat16
+I32 = mybir.dt.int32
+U32 = mybir.dt.uint32
+U8 = mybir.dt.uint8
+FP8X4 = mybir.dt.float8_e4m3fn_x4
+FP4X4 = mybir.dt.float4_e2m1fn_x4
+ALU = mybir.AluOpType
+ACT = mybir.ActivationFunctionType
+
+P = 128
+PACK = 4
+PASS_K = P * PACK
+PASSES = K // PASS_K
+HALF = 512
+HALVES = N // HALF
+ROW_TILES = T // P
+QUADS = 4
+QUAD = 32
+LIVE = 4
+WARM_PASSES = 14
+
+
+def tile_association_weighted_positions_k3_kernel(
+    tc, x_words, x_scales, a_words, a_scales, b_words, b_scales, d, r, out_0, out_1, out_2
+):
+    nc = tc.nc
+    with ExitStack() as ctx:
+        keep = ctx.enter_context(tc.tile_pool(name="keep", bufs=1))
+        psum = ctx.enter_context(tc.psum_pool(name="psum", bufs=8))
+        ctx.enter_context(tc.manual_schedule())
+
+        def kept(name, shape, dtype):
+            return keep.tile(shape, dtype, name=name, align_bytes=64)
+
+        xw = [kept("xw%d" % g, [P, T], U32) for g in range(PASSES)]
+        aw_first = kept("aw_first", [P, 1, 2 * HALF], U8)
+        aw_next = kept("aw_next", [P, PASSES - 1, 2 * HALF], U8)
+        aw_high = kept("aw_high", [P, PASSES, 2 * HALF], U8)
+        aw = {(0, 0): aw_first[:, 0, :]}
+        for g in range(1, PASSES):
+            aw[0, g] = aw_next[:, g - 1, :]
+        for g in range(PASSES):
+            aw[1, g] = aw_high[:, g, :]
+        bw = [kept("bw%d" % h, [P, PASSES, HALF], U32) for h in range(HALVES)]
+        xs = kept("xs", [P, PASSES, T], U8)
+        a_s = [kept("a_s%d" % h, [P, PASSES, HALF], U8) for h in range(HALVES)]
+        bs = kept("bs", [P, N], U8)
+        r_rows = kept("r_rows", [P, QUAD], BF16)
+        r_col = kept("r_col", [P, QUAD], BF16)
+        idle = kept("idle", [P, PACK * P], BF16)
+        idle_codes = kept("idle_codes", [P, P], U32)
+        idle_scale = kept("idle_scale", [P, P], U8)
+        ident = kept("ident", [P, P], F32)
+        warm = kept("warm", [P, 2], F32)
+        d_raw = {}
+        d_grp = {}
+        d_codes = {}
+        d_scale = {}
+        for h in range(HALVES):
+            for g in range(PASSES):
+                d_raw[h, g] = kept("d_raw%d%d" % (h, g), [P, PACK, HALF], BF16)
+                d_grp[h, g] = kept("d_grp%d%d" % (h, g), [P, HALF, PACK], BF16)
+                d_codes[h, g] = kept("d_codes%d%d" % (h, g), [P, HALF], U32)
+                d_scale[h, g] = kept("d_scale%d%d" % (h, g), [P, HALF], U8)
+        work = {}
+        y32 = {}
+        y16 = {}
+        for h in range(HALVES):
+            for i in range(ROW_TILES):
+                work[h, i] = kept("work%d%d" % (h, i), [P, HALF], F32)
+                y32[h, i] = kept("y32_%d%d" % (h, i), [P, HALF], F32)
+                y16[h, i] = kept("y16_%d%d" % (h, i), [P, HALF], BF16)
+        y_codes = [kept("y_codes%d" % h, [P, T], U32) for h in range(HALVES)]
+        y_scale = kept("y_scale", [P, T], U8)
+        y_grp = {}
+
+        def load_x(g):
+            nc.sync.dma_start(
+                out=xw[g][:].bitcast(I32),
+                in_=x_words[g].rearrange("p n t -> p (n t)").bitcast(I32),
+            )
+
+        def load_a(tile, h, first, last):
+            src = a_words[first:last].rearrange("g p n -> p g n")[:, :, 2 * HALF * h : 2 * HALF * (h + 1)]
+            nc.sync.dma_start(out=tile[:].bitcast(I32), in_=src.bitcast(I32))
+
+        def load_b(h):
+            src = b_words.rearrange("g p n t -> p g (n t)")[:, :, PACK * HALF * h : PACK * HALF * (h + 1)]
+            nc.sync.dma_start(out=bw[h][:].bitcast(I32), in_=src.bitcast(I32))
+
+        def load_d(h, g):
+            rows = d[PASS_K * g : PASS_K * (g + 1), HALF * h : HALF * (h + 1)]
+            nc.sync.dma_start(out=d_raw[h, g][:], in_=rows.rearrange("(p j) w -> p j w", j=PACK))
+
+        def load_plane(queue, plane, scales):
+            for q in range(QUADS):
+                rows = scales[:, LIVE * q : LIVE * (q + 1), :].rearrange("g r n -> r g n")
+                queue.dma_start(out=plane[QUAD * q : QUAD * q + LIVE].bitcast(I32), in_=rows.bitcast(I32))
+
+        def interleave_d(copy, h, g):
+            copy(
+                out=d_grp[h, g][:].rearrange("p (c i) t -> p c t i", i=4),
+                in_=d_raw[h, g][:].rearrange("p t (c i) -> p c t i", i=4),
+            )
+
+        def quantize_d(h, g):
+            nc.vector.quantize_mx(
+                out=d_codes[h, g][:].bitcast(FP8X4),
+                scales=d_scale[h, g][:],
+                in_=d_grp[h, g][:].rearrange("p c t -> p (c t)"),
+            )
+
+        def moving(kind, h, g):
+            if kind == "cross":
+                return aw[h, g].bitcast(FP4X4), a_s[h][:, g, :]
+            if kind == "pos":
+                return bw[h][:, g, :].bitcast(FP8X4), bs[LIVE * (g + 1) :, HALF * h : HALF * (h + 1)]
+            return d_codes[h, g][:].bitcast(FP8X4), d_scale[h, g][:]
+
+        def one_pass(bank, kind, h, i, g):
+            codes, scale = moving(kind, h, g)
+            nc.tensor.matmul_mx(
+                out=bank[:],
+                lhsT=xw[g][:, P * i : P * (i + 1)].bitcast(FP8X4),
+                lhsT_scale=xs[:, g, P * i : P * (i + 1)],
+                rhs=codes,
+                rhs_scale=scale,
+                start=(g == 0),
+                stop=(g == PASSES - 1),
+            )
+
+        def product(kind, h, i):
+            bank = psum.tile([P, HALF], F32, name="bank")
+            for g in range(PASSES):
+                one_pass(bank, kind, h, i, g)
+            return bank
+
+        def take_exp(bank, h, i):
+            nc.scalar.activation(out=work[h, i][:], in_=bank[:], func=ACT.Exp)
+
+        def cross(h, i):
+            take_exp(product("cross", h, i), h, i)
+
+        def pos(h, i):
+            bank = product("pos", h, i)
+            nc.vector.scalar_tensor_tensor(
+                out=work[h, i][:], in0=bank[:], scalar=r_col[:, i : i + 1], in1=work[h, i][:],
+                op0=ALU.mult, op1=ALU.mult,
+            )
+
+        def rest(h, i):
+            bank = product("rest", h, i)
+            nc.vector.tensor_tensor(out=y32[h, i][:], in0=bank[:], in1=work[h, i][:], op=ALU.add)
+            nc.sync.dma_start(out=out_0[P * i : P * (i + 1), HALF * h : HALF * (h + 1)], in_=y32[h, i][:])
+            nc.scalar.copy(
+                out=y16[h, i][:].rearrange("p (u q e) -> p u q e", u=2, e=2),
+                in_=y32[h, i][:].rearrange("p (q u e) -> p u q e", u=2, e=2),
+            )
+
+        def last_rest(h, i):
+            quarter = HALF // 2
+            banks = []
+            for c in range(2):
+                bank = psum.tile([P, quarter], F32, name="bank")
+                cols = slice(quarter * c, quarter * (c + 1))
+                for g in range(PASSES):
+                    nc.tensor.matmul_mx(
+                        out=bank[:],
+                        lhsT=xw[g][:, P * i : P * (i + 1)].bitcast(FP8X4),
+                        lhsT_scale=xs[:, g, P * i : P * (i + 1)],
+                        rhs=d_codes[h, g][:, cols].bitcast(FP8X4),
+                        rhs_scale=d_scale[h, g][:, cols],
+                        start=(g == 0),
+                        stop=(g == PASSES - 1),
+                    )
+                banks.append(bank)
+            sorted16 = y16[h, i][:].rearrange("p (u q e) -> p u q e", u=2, e=2)
+
+            def by_pairs(ap):
+                return ap.rearrange("p (q u e) -> p u q e", u=2, e=2)
+
+            low, high = slice(0, quarter), slice(quarter, HALF)
+            nc.vector.tensor_tensor(out=y32[h, i][:, low], in0=banks[0][:], in1=work[h, i][:, low], op=ALU.add)
+            nc.scalar.copy(out=sorted16[:, :, 0 : P // 2, :], in_=by_pairs(y32[h, i][:, low]))
+            nc.vector.tensor_tensor(
+                out=sorted16[:, :, P // 2 : P, :], in0=by_pairs(banks[1][:]), in1=by_pairs(work[h, i][:, high]), op=ALU.add
+            )
+            nc.vector.tensor_tensor(out=y32[h, i][:, high], in0=banks[1][:], in1=work[h, i][:, high], op=ALU.add)
+            nc.sync.dma_start(out=out_0[P * i : P * (i + 1), HALF * h : HALF * (h + 1)], in_=y32[h, i][:])
+
+        def turn(h, tiles):
+            bank = psum.tile([P, 2, 2, P], F32, name="bank")
+            for j, i in enumerate(tiles):
+                pairs = y16[h, i][:].bitcast(F32)
+                for u in range(2):
+                    nc.tensor.transpose(bank[:, j, u, :], pairs[:, P * u : P * (u + 1)], ident[:])
+            return bank
+
+        def gather(bank, h, tiles, copy=nc.scalar.copy):
+            n = len(tiles)
+            y_grp[h, tiles[0]] = kept("y_grp%d%d" % (h, tiles[0]), [P, n * P * PACK], BF16)
+            copy(
+                out=y_grp[h, tiles[0]][:].bitcast(F32).rearrange("p (j m u) -> p j m u", j=n, u=2),
+                in_=bank[:, 0:n].rearrange("p j u m -> p j m u"),
+            )
+
+        def quantize_y(h, tiles):
+            cols = slice(P * tiles[0], P * (tiles[-1] + 1))
+            nc.vector.quantize_mx(
+                out=y_codes[h][:, cols].bitcast(FP8X4),
+                scales=y_scale[LIVE * h :, cols],
+                in_=y_grp[h, tiles[0]][:],
+            )
+
+        def store_words(queue, h, first, last):
+            dst = out_1[h].rearrange("p m t -> p (m t)")[:, PACK * P * first : PACK * P * last]
+            queue.dma_start(out=dst.bitcast(I32), in_=y_codes[h][:, P * first : P * last].bitcast(I32))
+
+        def store_scales(queue, q):
+            queue.dma_start(
+                out=out_2[:, LIVE * q : LIVE * (q + 1), :].bitcast(I32),
+                in_=y_scale[QUAD * q : QUAD * q + LIVE * HALVES, :].bitcast(I32),
+            )
+
+        nc.vector.memset(xs[:].bitcast(I32), 0)
+        nc.vector.memset(a_s[0][:].bitcast(I32), 0)
+        nc.gpsimd.memset(bs[:].bitcast(I32), 0)
+        nc.gpsimd.memset(r_rows[:], 0.0)
+        load_a(aw_first, 0, 0, 1)
+        load_x(0)
+        load_plane(nc.sync, xs, x_scales)
+        load_plane(nc.scalar, a_s[0], a_scales[:, :, 0:HALF])
+        nc.vector.memset(idle[:], 1.0)
+        nc.vector.memset(warm[:], 0.0)
+        nc.vector.quantize_mx(out=idle_codes[:].bitcast(FP8X4), scales=idle_scale[:], in_=idle[:])
+        nc.scalar.activation(out=warm[:, 1:2], in_=warm[:, 0:1], func=ACT.Exp)
+        for q in range(QUADS):
+            nc.gpsimd.dma_start(
+                out=bs[QUAD * q + LIVE : QUAD * q + LIVE * (PASSES + 1), :].bitcast(I32),
+                in_=b_scales[:, LIVE * q : LIVE * (q + 1), :].bitcast(I32),
+            )
+        for q in range(QUADS):
+            nc.gpsimd.dma_start(
+                out=r_rows[QUAD * q : QUAD * q + ROW_TILES, :],
+                in_=r.rearrange("(i q a) -> q i a", q=QUADS, a=QUAD)[q],
+            )
+        make_identity(nc, ident[:])
+        nc.vector.memset(a_s[1][:].bitcast(I32), 0)
+        spare = psum.tile([P, P], F32, name="bank")
+        for step in range(WARM_PASSES):
+            nc.tensor.matmul_mx(
+                out=spare[:], lhsT=idle_codes[:].bitcast(FP8X4), lhsT_scale=idle_scale[:],
+                rhs=idle_codes[:].bitcast(FP8X4), rhs_scale=idle_scale[:], start=True, stop=True,
+            )
+        load_x(1)
+        load_a(aw_next, 0, 1, PASSES)
+        load_x(2)
+        load_a(aw_high, 1, 0, PASSES)
+        load_plane(nc.sync, a_s[1], a_scales[:, :, HALF:N])
+        for g in range(PASSES):
+            load_d(0, g)
+        load_b(0)
+        load_d(1, 0)
+        load_d(1, 1)
+        load_d(1, 2)
+        load_b(1)
+
+        banks = [psum.tile([P, HALF], F32, name="bank") for i in range(ROW_TILES)]
+        for g in range(PASSES):
+            for i in range(ROW_TILES):
+                one_pass(banks[i], "cross", 0, i, g)
+        for i in range(ROW_TILES):
+            take_exp(banks[i], 0, i)
+
+        interleave_d(nc.vector.tensor_copy, 0, 0)
+        interleave_d(nc.vector.tensor_copy, 0, 1)
+        quantize_d(0, 0)
+        interleave_d(nc.vector.tensor_copy, 0, 2)
+        quantize_d(0, 1)
+        nc.vector.transpose(out=r_col[:], in_=r_rows[:])
+        for i in range(ROW_TILES):
+            cross(1, i)
+
+        pos(0, 0)
+        quantize_d(0, 2)
+        pos(0, 1)
+        interleave_d(nc.vector.tensor_copy, 1, 0)
+        interleave_d(nc.scalar.copy, 1, 1)
+        interleave_d(nc.scalar.copy, 1, 2)
+        pos(0, 2)
+        pos(0, 3)
+        quantize_d(1, 0)
+        pos(0, 4)
+        pos(0, 5)
+        quantize_d(1, 1)
+
+        pos(1, 0)
+        rest(0, 0)
+        quantize_d(1, 2)
+        rest(0, 1)
+        pos(1, 1)
+        rest(0, 2)
+        rest(0, 3)
+        pos(1, 2)
+        rest(0, 4)
+        rest(0, 5)
+        pos(1, 3)
+        rest(1, 0)
+        groups = [[0, 1], [2, 3], [4, 5]]
+        turned = [turn(0, tiles) for tiles in groups]
+        gather(turned[0], 0, groups[0])
+        gather(turned[1], 0, groups[1])
+        rest(1, 1)
+        gather(turned[2], 0, groups[2])
+        quantize_y(0, groups[0])
+        pos(1, 4)
+        quantize_y(0, groups[1])
+        rest(1, 2)
+        quantize_y(0, groups[2])
+        store_words(nc.sync, 0, 0, ROW_TILES)
+        rest(1, 3)
+        rest(1, 4)
+        first = turn(1, [0, 1])
+        second = turn(1, [2])
+        gather(first, 1, [0, 1])
+        gather(second, 1, [2])
+        pos(1, 5)
+        quantize_y(1, [0, 1])
+        last_rest(1, 5)
+        quantize_y(1, [2])
+        store_words(nc.sync, 1, 0, 3)
+        first = turn(1, [3, 4])
+        second = turn(1, [5])
+        gather(first, 1, [3, 4])
+        gather(second, 1, [5], nc.vector.tensor_copy)
+        quantize_y(1, [3, 4])
+        quantize_y(1, [5])
+        store_words(nc.sync, 1, 3, ROW_TILES)
+        for q in range(QUADS):
+            store_scales(nc.scalar if q % 2 else nc.sync, q)

@@ -23,10 +23,12 @@ PASSES = K // PASS_K
 HALF = 512
 HALVES = N // HALF
 ROW_TILES = T // P
-QUADS = 4
 QUAD = 32
+QUADS = P // QUAD
 LIVE = 4
-WARM_PASSES = 14
+BANKS = 8
+ALIGN = 256
+SHIFT = 32
 
 
 def tile_association_weighted_positions_k3_kernel(
@@ -35,167 +37,161 @@ def tile_association_weighted_positions_k3_kernel(
     nc = tc.nc
     with ExitStack() as ctx:
         keep = ctx.enter_context(tc.tile_pool(name="keep", bufs=1))
-        psum = ctx.enter_context(tc.psum_pool(name="psum", bufs=8))
+        psum = ctx.enter_context(tc.psum_pool(name="psum", bufs=BANKS))
         ctx.enter_context(tc.manual_schedule())
 
         def kept(name, shape, dtype):
-            return keep.tile(shape, dtype, name=name, align_bytes=64)
+            return keep.tile(shape, dtype, name=name, align_bytes=ALIGN)
 
-        xw = [kept("xw%d" % g, [P, T], U32) for g in range(PASSES)]
-        aw_first = kept("aw_first", [P, 1, 2 * HALF], U8)
-        aw_next = kept("aw_next", [P, PASSES - 1, 2 * HALF], U8)
-        aw_high = kept("aw_high", [P, PASSES, 2 * HALF], U8)
-        aw = {(0, 0): aw_first[:, 0, :]}
+        x_codes = [kept("x_codes%d" % g, [P, SHIFT + T], U32)[:, SHIFT:] for g in range(PASSES)]
+        a_first = kept("a_first", [P, 1, 2 * HALF], U8)
+        a_next = kept("a_next", [P, PASSES - 1, 2 * HALF], U8)
+        a_high = kept("a_high", [P, PASSES, 2 * HALF], U8)
+        a_codes = {(0, 0): a_first[:, 0, :]}
         for g in range(1, PASSES):
-            aw[0, g] = aw_next[:, g - 1, :]
+            a_codes[0, g] = a_next[:, g - 1, :]
         for g in range(PASSES):
-            aw[1, g] = aw_high[:, g, :]
-        bw = [kept("bw%d" % h, [P, PASSES, HALF], U32) for h in range(HALVES)]
-        xs = kept("xs", [P, PASSES, T], U8)
-        a_s = [kept("a_s%d" % h, [P, PASSES, HALF], U8) for h in range(HALVES)]
-        bs = kept("bs", [P, N], U8)
+            a_codes[1, g] = a_high[:, g, :]
+        b_codes = [kept("b_codes%d" % h, [P, PASSES, HALF], U32) for h in range(HALVES)]
+        x_plane = kept("x_plane", [P, PASSES, T], U8)
+        a_plane = [kept("a_plane%d" % h, [P, PASSES, HALF], U8) for h in range(HALVES)]
+        b_planes = kept("b_planes", [P, N], U8)
         r_rows = kept("r_rows", [P, QUAD], BF16)
-        r_col = kept("r_col", [P, QUAD], BF16)
-        idle = kept("idle", [P, PACK * P], BF16)
-        idle_codes = kept("idle_codes", [P, P], U32)
-        idle_scale = kept("idle_scale", [P, P], U8)
+        r_cols = kept("r_cols", [P, QUAD], BF16)
         ident = kept("ident", [P, P], F32)
-        warm = kept("warm", [P, 2], F32)
-        d_raw = {}
-        d_grp = {}
-        d_codes = {}
-        d_scale = {}
+        d_rows, d_fours, d_codes, d_plane = {}, {}, {}, {}
         for h in range(HALVES):
             for g in range(PASSES):
-                d_raw[h, g] = kept("d_raw%d%d" % (h, g), [P, PACK, HALF], BF16)
-                d_grp[h, g] = kept("d_grp%d%d" % (h, g), [P, HALF, PACK], BF16)
+                d_rows[h, g] = kept("d_rows%d%d" % (h, g), [P, PACK, HALF], BF16)
+        for h in range(HALVES):
+            for g in range(PASSES):
+                d_fours[h, g] = kept("d_fours%d%d" % (h, g), [P, HALF, PACK], BF16)
                 d_codes[h, g] = kept("d_codes%d%d" % (h, g), [P, HALF], U32)
-                d_scale[h, g] = kept("d_scale%d%d" % (h, g), [P, HALF], U8)
-        work = {}
-        y32 = {}
-        y16 = {}
+                d_plane[h, g] = kept("d_plane%d%d" % (h, g), [P, HALF], U8)
+        weighted, y32, y16, y_fours = {}, {}, {}, {}
         for h in range(HALVES):
             for i in range(ROW_TILES):
-                work[h, i] = kept("work%d%d" % (h, i), [P, HALF], F32)
+                weighted[h, i] = kept("weighted%d%d" % (h, i), [P, HALF], F32)
                 y32[h, i] = kept("y32_%d%d" % (h, i), [P, HALF], F32)
                 y16[h, i] = kept("y16_%d%d" % (h, i), [P, HALF], BF16)
         y_codes = [kept("y_codes%d" % h, [P, T], U32) for h in range(HALVES)]
-        y_scale = kept("y_scale", [P, T], U8)
-        y_grp = {}
+        y_planes = kept("y_planes", [P, T], U8)
+
 
         def load_x(g):
-            nc.sync.dma_start(
-                out=xw[g][:].bitcast(I32),
-                in_=x_words[g].rearrange("p n t -> p (n t)").bitcast(I32),
-            )
+            src = x_words[g].rearrange("p n t -> p (n t)")
+            nc.sync.dma_start(out=x_codes[g].bitcast(I32), in_=src.bitcast(I32))
 
-        def load_a(tile, h, first, last):
-            src = a_words[first:last].rearrange("g p n -> p g n")[:, :, 2 * HALF * h : 2 * HALF * (h + 1)]
+        def load_a(tile, h, first_pass, end_pass):
+            src = a_words[first_pass:end_pass].rearrange("g p n -> p g n")[:, :, 2 * HALF * h : 2 * HALF * (h + 1)]
             nc.sync.dma_start(out=tile[:].bitcast(I32), in_=src.bitcast(I32))
 
         def load_b(h):
             src = b_words.rearrange("g p n t -> p g (n t)")[:, :, PACK * HALF * h : PACK * HALF * (h + 1)]
-            nc.sync.dma_start(out=bw[h][:].bitcast(I32), in_=src.bitcast(I32))
+            nc.sync.dma_start(out=b_codes[h][:].bitcast(I32), in_=src.bitcast(I32))
 
         def load_d(h, g):
             rows = d[PASS_K * g : PASS_K * (g + 1), HALF * h : HALF * (h + 1)]
-            nc.sync.dma_start(out=d_raw[h, g][:], in_=rows.rearrange("(p j) w -> p j w", j=PACK))
+            nc.sync.dma_start(out=d_rows[h, g][:], in_=rows.rearrange("(p j) w -> p j w", j=PACK))
 
-        def load_plane(queue, plane, scales):
-            for q in range(QUADS):
-                rows = scales[:, LIVE * q : LIVE * (q + 1), :].rearrange("g r n -> r g n")
-                queue.dma_start(out=plane[QUAD * q : QUAD * q + LIVE].bitcast(I32), in_=rows.bitcast(I32))
+        def load_plane(plane, scales, live_rows):
+            for j in live_rows:
+                rows = scales.rearrange("g (q j) n -> j q g n", j=LIVE)[j]
+                nc.sync.dma_start(out=plane[j:P:QUAD].bitcast(I32), in_=rows.bitcast(I32))
+
 
         def interleave_d(copy, h, g):
-            copy(
-                out=d_grp[h, g][:].rearrange("p (c i) t -> p c t i", i=4),
-                in_=d_raw[h, g][:].rearrange("p t (c i) -> p c t i", i=4),
-            )
+            copy(out=d_fours[h, g][:], in_=d_rows[h, g][:].rearrange("p t c -> p c t"))
 
         def quantize_d(h, g):
             nc.vector.quantize_mx(
                 out=d_codes[h, g][:].bitcast(FP8X4),
-                scales=d_scale[h, g][:],
-                in_=d_grp[h, g][:].rearrange("p c t -> p (c t)"),
+                scales=d_plane[h, g][:],
+                in_=d_fours[h, g][:].rearrange("p c t -> p (c t)"),
             )
 
-        def moving(kind, h, g):
-            if kind == "cross":
-                return aw[h, g].bitcast(FP4X4), a_s[h][:, g, :]
-            if kind == "pos":
-                return bw[h][:, g, :].bitcast(FP8X4), bs[LIVE * (g + 1) :, HALF * h : HALF * (h + 1)]
-            return d_codes[h, g][:].bitcast(FP8X4), d_scale[h, g][:]
 
-        def one_pass(bank, kind, h, i, g):
-            codes, scale = moving(kind, h, g)
+        def operand_a(h, g):
+            return a_codes[h, g].bitcast(FP4X4), a_plane[h][:, g, :]
+
+        def operand_b(h, g):
+            return b_codes[h][:, g, :].bitcast(FP8X4), b_planes[LIVE * (g + 1) :, HALF * h : HALF * (h + 1)]
+
+        def operand_d(h, g, cols=slice(0, HALF)):
+            return d_codes[h, g][:, cols].bitcast(FP8X4), d_plane[h, g][:, cols]
+
+        def one_pass(bank, operand, i, g):
+            codes, plane = operand
             nc.tensor.matmul_mx(
                 out=bank[:],
-                lhsT=xw[g][:, P * i : P * (i + 1)].bitcast(FP8X4),
-                lhsT_scale=xs[:, g, P * i : P * (i + 1)],
+                lhsT=x_codes[g][:, P * i : P * (i + 1)].bitcast(FP8X4),
+                lhsT_scale=x_plane[:, g, P * i : P * (i + 1)],
                 rhs=codes,
-                rhs_scale=scale,
+                rhs_scale=plane,
                 start=(g == 0),
                 stop=(g == PASSES - 1),
             )
 
-        def product(kind, h, i):
+        def product(operand_of, h, i):
             bank = psum.tile([P, HALF], F32, name="bank")
             for g in range(PASSES):
-                one_pass(bank, kind, h, i, g)
+                one_pass(bank, operand_of(h, g), i, g)
             return bank
 
         def take_exp(bank, h, i):
-            nc.scalar.activation(out=work[h, i][:], in_=bank[:], func=ACT.Exp)
+            nc.scalar.activation(out=weighted[h, i][:], in_=bank[:], func=ACT.Exp)
 
         def cross(h, i):
-            take_exp(product("cross", h, i), h, i)
+            take_exp(product(operand_a, h, i), h, i)
 
         def pos(h, i):
-            bank = product("pos", h, i)
+            bank = product(operand_b, h, i)
             nc.vector.scalar_tensor_tensor(
-                out=work[h, i][:], in0=bank[:], scalar=r_col[:, i : i + 1], in1=work[h, i][:],
-                op0=ALU.mult, op1=ALU.mult,
+                out=weighted[h, i][:],
+                in0=bank[:],
+                scalar=r_cols[:, i : i + 1],
+                in1=weighted[h, i][:],
+                op0=ALU.mult,
+                op1=ALU.mult,
             )
+
+        def store_y(h, i):
+            nc.sync.dma_start(out=out_0[P * i : P * (i + 1), HALF * h : HALF * (h + 1)], in_=y32[h, i][:])
 
         def rest(h, i):
-            bank = product("rest", h, i)
-            nc.vector.tensor_tensor(out=y32[h, i][:], in0=bank[:], in1=work[h, i][:], op=ALU.add)
-            nc.sync.dma_start(out=out_0[P * i : P * (i + 1), HALF * h : HALF * (h + 1)], in_=y32[h, i][:])
-            nc.scalar.copy(
-                out=y16[h, i][:].rearrange("p (u q e) -> p u q e", u=2, e=2),
-                in_=y32[h, i][:].rearrange("p (q u e) -> p u q e", u=2, e=2),
-            )
+            bank = product(operand_d, h, i)
+            nc.vector.tensor_tensor(out=y32[h, i][:], in0=bank[:], in1=weighted[h, i][:], op=ALU.add)
+            store_y(h, i)
+
+
+        def by_pairs(ap):
+            return ap.rearrange("p (q u e) -> p u q e", u=2, e=2)
+
+        def sorted_pairs(h, i):
+            return y16[h, i][:].rearrange("p (u q e) -> p u q e", u=2, e=2)
+
+        def round_y(h, i):
+            nc.scalar.copy(out=sorted_pairs(h, i), in_=by_pairs(y32[h, i][:]))
 
         def last_rest(h, i):
-            quarter = HALF // 2
-            banks = []
+            width = HALF // 2
+            parts = []
             for c in range(2):
-                bank = psum.tile([P, quarter], F32, name="bank")
-                cols = slice(quarter * c, quarter * (c + 1))
+                cols = slice(width * c, width * (c + 1))
+                bank = psum.tile([P, width], F32, name="bank")
                 for g in range(PASSES):
-                    nc.tensor.matmul_mx(
-                        out=bank[:],
-                        lhsT=xw[g][:, P * i : P * (i + 1)].bitcast(FP8X4),
-                        lhsT_scale=xs[:, g, P * i : P * (i + 1)],
-                        rhs=d_codes[h, g][:, cols].bitcast(FP8X4),
-                        rhs_scale=d_scale[h, g][:, cols],
-                        start=(g == 0),
-                        stop=(g == PASSES - 1),
-                    )
-                banks.append(bank)
-            sorted16 = y16[h, i][:].rearrange("p (u q e) -> p u q e", u=2, e=2)
-
-            def by_pairs(ap):
-                return ap.rearrange("p (q u e) -> p u q e", u=2, e=2)
-
-            low, high = slice(0, quarter), slice(quarter, HALF)
-            nc.vector.tensor_tensor(out=y32[h, i][:, low], in0=banks[0][:], in1=work[h, i][:, low], op=ALU.add)
-            nc.scalar.copy(out=sorted16[:, :, 0 : P // 2, :], in_=by_pairs(y32[h, i][:, low]))
-            nc.vector.tensor_tensor(
-                out=sorted16[:, :, P // 2 : P, :], in0=by_pairs(banks[1][:]), in1=by_pairs(work[h, i][:, high]), op=ALU.add
-            )
-            nc.vector.tensor_tensor(out=y32[h, i][:, high], in0=banks[1][:], in1=work[h, i][:, high], op=ALU.add)
-            nc.sync.dma_start(out=out_0[P * i : P * (i + 1), HALF * h : HALF * (h + 1)], in_=y32[h, i][:])
+                    one_pass(bank, operand_d(h, g, cols), i, g)
+                parts.append((bank, cols))
+            for c, (bank, cols) in enumerate(parts):
+                nc.vector.tensor_tensor(
+                    out=sorted_pairs(h, i)[:, :, P // 2 * c : P // 2 * (c + 1), :],
+                    in0=by_pairs(bank[:]),
+                    in1=by_pairs(weighted[h, i][:, cols]),
+                    op=ALU.add,
+                )
+            for bank, cols in parts:
+                nc.vector.tensor_tensor(out=y32[h, i][:, cols], in0=bank[:], in1=weighted[h, i][:, cols], op=ALU.add)
+            store_y(h, i)
 
         def turn(h, tiles):
             bank = psum.tile([P, 2, 2, P], F32, name="bank")
@@ -205,47 +201,45 @@ def tile_association_weighted_positions_k3_kernel(
                     nc.tensor.transpose(bank[:, j, u, :], pairs[:, P * u : P * (u + 1)], ident[:])
             return bank
 
-        def gather(bank, h, tiles, copy=nc.scalar.copy):
-            n = len(tiles)
-            y_grp[h, tiles[0]] = kept("y_grp%d%d" % (h, tiles[0]), [P, n * P * PACK], BF16)
-            copy(
-                out=y_grp[h, tiles[0]][:].bitcast(F32).rearrange("p (j m u) -> p j m u", j=n, u=2),
-                in_=bank[:, 0:n].rearrange("p j u m -> p j m u"),
+        def join_pairs(bank, h, tiles):
+            count = len(tiles)
+            y_fours[h, tiles[0]] = kept("y_fours%d%d" % (h, tiles[0]), [P, count * P * PACK], BF16)
+            nc.scalar.copy(
+                out=y_fours[h, tiles[0]][:].bitcast(F32).rearrange("p (j m u) -> p j m u", j=count, u=2),
+                in_=bank[:, 0:count].rearrange("p j u m -> p j m u"),
             )
 
         def quantize_y(h, tiles):
-            cols = slice(P * tiles[0], P * (tiles[-1] + 1))
+            tracks = slice(P * tiles[0], P * (tiles[-1] + 1))
             nc.vector.quantize_mx(
-                out=y_codes[h][:, cols].bitcast(FP8X4),
-                scales=y_scale[LIVE * h :, cols],
-                in_=y_grp[h, tiles[0]][:],
+                out=y_codes[h][:, tracks].bitcast(FP8X4),
+                scales=y_planes[LIVE * h :, tracks],
+                in_=y_fours[h, tiles[0]][:],
             )
 
-        def store_words(queue, h, first, last):
-            dst = out_1[h].rearrange("p m t -> p (m t)")[:, PACK * P * first : PACK * P * last]
-            queue.dma_start(out=dst.bitcast(I32), in_=y_codes[h][:, P * first : P * last].bitcast(I32))
+        def store_words(h, first_tile, end_tile):
+            dst = out_1[h].rearrange("p m t -> p (m t)")[:, PACK * P * first_tile : PACK * P * end_tile]
+            nc.sync.dma_start(out=dst.bitcast(I32), in_=y_codes[h][:, P * first_tile : P * end_tile].bitcast(I32))
 
         def store_scales(queue, q):
             queue.dma_start(
                 out=out_2[:, LIVE * q : LIVE * (q + 1), :].bitcast(I32),
-                in_=y_scale[QUAD * q : QUAD * q + LIVE * HALVES, :].bitcast(I32),
+                in_=y_planes[QUAD * q : QUAD * q + LIVE * HALVES, :].bitcast(I32),
             )
 
-        nc.vector.memset(xs[:].bitcast(I32), 0)
-        nc.vector.memset(a_s[0][:].bitcast(I32), 0)
-        nc.gpsimd.memset(bs[:].bitcast(I32), 0)
-        nc.gpsimd.memset(r_rows[:], 0.0)
-        load_a(aw_first, 0, 0, 1)
+        nc.vector.memset(a_plane[0][:].bitcast(I32), 0)
+        nc.vector.memset(x_plane[:].bitcast(I32), 0)
+        load_a(a_first, 0, 0, 1)
+        load_plane(a_plane[0], a_scales[:, :, 0:HALF], range(1))
         load_x(0)
-        load_plane(nc.sync, xs, x_scales)
-        load_plane(nc.scalar, a_s[0], a_scales[:, :, 0:HALF])
-        nc.vector.memset(idle[:], 1.0)
-        nc.vector.memset(warm[:], 0.0)
-        nc.vector.quantize_mx(out=idle_codes[:].bitcast(FP8X4), scales=idle_scale[:], in_=idle[:])
-        nc.scalar.activation(out=warm[:, 1:2], in_=warm[:, 0:1], func=ACT.Exp)
+        load_plane(a_plane[0], a_scales[:, :, 0:HALF], range(1, LIVE))
+        load_plane(x_plane, x_scales, range(LIVE))
+
+        nc.gpsimd.memset(b_planes[:].bitcast(I32), 0)
+        nc.gpsimd.memset(r_rows[:], 0.0)
         for q in range(QUADS):
             nc.gpsimd.dma_start(
-                out=bs[QUAD * q + LIVE : QUAD * q + LIVE * (PASSES + 1), :].bitcast(I32),
+                out=b_planes[QUAD * q + LIVE : QUAD * q + LIVE * (PASSES + 1), :].bitcast(I32),
                 in_=b_scales[:, LIVE * q : LIVE * (q + 1), :].bitcast(I32),
             )
         for q in range(QUADS):
@@ -254,96 +248,89 @@ def tile_association_weighted_positions_k3_kernel(
                 in_=r.rearrange("(i q a) -> q i a", q=QUADS, a=QUAD)[q],
             )
         make_identity(nc, ident[:])
-        nc.vector.memset(a_s[1][:].bitcast(I32), 0)
-        spare = psum.tile([P, P], F32, name="bank")
-        for step in range(WARM_PASSES):
-            nc.tensor.matmul_mx(
-                out=spare[:], lhsT=idle_codes[:].bitcast(FP8X4), lhsT_scale=idle_scale[:],
-                rhs=idle_codes[:].bitcast(FP8X4), rhs_scale=idle_scale[:], start=True, stop=True,
-            )
+
+        nc.vector.memset(a_plane[1][:].bitcast(I32), 0)
         load_x(1)
-        load_a(aw_next, 0, 1, PASSES)
+        load_a(a_next, 0, 1, PASSES)
         load_x(2)
-        load_a(aw_high, 1, 0, PASSES)
-        load_plane(nc.sync, a_s[1], a_scales[:, :, HALF:N])
-        for g in range(PASSES):
-            load_d(0, g)
+        load_a(a_high, 1, 0, PASSES)
+        load_plane(a_plane[1], a_scales[:, :, HALF:N], range(LIVE))
+        load_d(0, 0)
+        load_d(0, 1)
         load_b(0)
+        load_d(0, 2)
         load_d(1, 0)
+        load_b(1)
         load_d(1, 1)
         load_d(1, 2)
-        load_b(1)
 
         banks = [psum.tile([P, HALF], F32, name="bank") for i in range(ROW_TILES)]
         for g in range(PASSES):
             for i in range(ROW_TILES):
-                one_pass(banks[i], "cross", 0, i, g)
+                one_pass(banks[i], operand_a(0, g), i, g)
         for i in range(ROW_TILES):
             take_exp(banks[i], 0, i)
-
-        interleave_d(nc.vector.tensor_copy, 0, 0)
-        interleave_d(nc.vector.tensor_copy, 0, 1)
-        quantize_d(0, 0)
-        interleave_d(nc.vector.tensor_copy, 0, 2)
-        quantize_d(0, 1)
-        nc.vector.transpose(out=r_col[:], in_=r_rows[:])
         for i in range(ROW_TILES):
             cross(1, i)
 
+        interleave_d(nc.vector.tensor_copy, 0, 0)
+        quantize_d(0, 0)
+        interleave_d(nc.vector.tensor_copy, 0, 1)
+        nc.vector.transpose(out=r_cols[:], in_=r_rows[:])
+        quantize_d(0, 1)
+        interleave_d(nc.vector.tensor_copy, 0, 2)
+
         pos(0, 0)
         quantize_d(0, 2)
-        pos(0, 1)
-        interleave_d(nc.vector.tensor_copy, 1, 0)
-        interleave_d(nc.scalar.copy, 1, 1)
-        interleave_d(nc.scalar.copy, 1, 2)
-        pos(0, 2)
-        pos(0, 3)
-        quantize_d(1, 0)
-        pos(0, 4)
-        pos(0, 5)
-        quantize_d(1, 1)
+        for g in range(PASSES):
+            interleave_d(nc.scalar.copy, 1, g)
+        for i in range(1, ROW_TILES):
+            pos(0, i)
 
-        pos(1, 0)
-        rest(0, 0)
-        quantize_d(1, 2)
-        rest(0, 1)
-        pos(1, 1)
-        rest(0, 2)
-        rest(0, 3)
-        pos(1, 2)
-        rest(0, 4)
-        rest(0, 5)
+        for step in range(PASSES):
+            pos(1, step)
+            quantize_d(1, step)
+            for i in (2 * step, 2 * step + 1):
+                rest(0, i)
+                round_y(0, i)
         pos(1, 3)
         rest(1, 0)
-        groups = [[0, 1], [2, 3], [4, 5]]
-        turned = [turn(0, tiles) for tiles in groups]
-        gather(turned[0], 0, groups[0])
-        gather(turned[1], 0, groups[1])
+        round_y(1, 0)
         rest(1, 1)
-        gather(turned[2], 0, groups[2])
-        quantize_y(0, groups[0])
+
+        twos = [[0, 1], [2, 3], [4, 5]]
+        turned = [turn(0, tiles) for tiles in twos]
+        join_pairs(turned[0], 0, twos[0])
+        round_y(1, 1)
+        join_pairs(turned[1], 0, twos[1])
+        join_pairs(turned[2], 0, twos[2])
         pos(1, 4)
-        quantize_y(0, groups[1])
+        quantize_y(0, twos[0])
         rest(1, 2)
-        quantize_y(0, groups[2])
-        store_words(nc.sync, 0, 0, ROW_TILES)
+        round_y(1, 2)
+        quantize_y(0, twos[1])
         rest(1, 3)
+        round_y(1, 3)
+        quantize_y(0, twos[2])
+        store_words(0, 0, ROW_TILES)
         rest(1, 4)
-        first = turn(1, [0, 1])
-        second = turn(1, [2])
-        gather(first, 1, [0, 1])
-        gather(second, 1, [2])
+
+        turned = [turn(1, [0, 1]), turn(1, [2])]
+        join_pairs(turned[0], 1, [0, 1])
+        round_y(1, 4)
+        join_pairs(turned[1], 1, [2])
         pos(1, 5)
         quantize_y(1, [0, 1])
+        store_words(1, 0, 2)
         last_rest(1, 5)
+
+        turned = [turn(1, [3, 4]), turn(1, [5])]
+        join_pairs(turned[0], 1, [3, 4])
+        join_pairs(turned[1], 1, [5])
         quantize_y(1, [2])
-        store_words(nc.sync, 1, 0, 3)
-        first = turn(1, [3, 4])
-        second = turn(1, [5])
-        gather(first, 1, [3, 4])
-        gather(second, 1, [5], nc.vector.tensor_copy)
         quantize_y(1, [3, 4])
+        store_words(1, 2, 5)
         quantize_y(1, [5])
-        store_words(nc.sync, 1, 3, ROW_TILES)
+        store_words(1, 5, ROW_TILES)
         for q in range(QUADS):
             store_scales(nc.scalar if q % 2 else nc.sync, q)

from contextlib import ExitStack

import concourse.mybir as mybir
from concourse.masks import make_identity

T, K, N = 768, 1536, 1024
FLOPS = 3 * 2 * T * K * N

F32 = mybir.dt.float32
BF16 = mybir.dt.bfloat16
I32 = mybir.dt.int32
U32 = mybir.dt.uint32
U8 = mybir.dt.uint8
FP8X4 = mybir.dt.float8_e4m3fn_x4
FP4X4 = mybir.dt.float4_e2m1fn_x4
ALU = mybir.AluOpType
ACT = mybir.ActivationFunctionType

P = 128
PACK = 4
PASS_K = P * PACK
PASSES = K // PASS_K
HALF = 512
HALVES = N // HALF
ROW_TILES = T // P
QUAD = 32
QUADS = P // QUAD
LIVE = 4
BANKS = 8
ALIGN = 256
SHIFT = 32


def tile_association_weighted_positions_k3_kernel(
    tc, x_words, x_scales, a_words, a_scales, b_words, b_scales, d, r, out_0, out_1, out_2
):
    nc = tc.nc
    with ExitStack() as ctx:
        keep = ctx.enter_context(tc.tile_pool(name="keep", bufs=1))
        psum = ctx.enter_context(tc.psum_pool(name="psum", bufs=BANKS))
        ctx.enter_context(tc.manual_schedule())

        def kept(name, shape, dtype):
            return keep.tile(shape, dtype, name=name, align_bytes=ALIGN)

        x_codes = [kept("x_codes%d" % g, [P, SHIFT + T], U32)[:, SHIFT:] for g in range(PASSES)]
        a_first = kept("a_first", [P, 1, 2 * HALF], U8)
        a_next = kept("a_next", [P, PASSES - 1, 2 * HALF], U8)
        a_high = kept("a_high", [P, PASSES, 2 * HALF], U8)
        a_codes = {(0, 0): a_first[:, 0, :]}
        for g in range(1, PASSES):
            a_codes[0, g] = a_next[:, g - 1, :]
        for g in range(PASSES):
            a_codes[1, g] = a_high[:, g, :]
        b_codes = [kept("b_codes%d" % h, [P, PASSES, HALF], U32) for h in range(HALVES)]
        x_plane = kept("x_plane", [P, PASSES, T], U8)
        a_plane = [kept("a_plane%d" % h, [P, PASSES, HALF], U8) for h in range(HALVES)]
        b_planes = kept("b_planes", [P, N], U8)
        r_rows = kept("r_rows", [P, QUAD], BF16)
        r_cols = kept("r_cols", [P, QUAD], BF16)
        ident = kept("ident", [P, P], F32)
        d_rows, d_fours, d_codes, d_plane = {}, {}, {}, {}
        for h in range(HALVES):
            for g in range(PASSES):
                d_rows[h, g] = kept("d_rows%d%d" % (h, g), [P, PACK, HALF], BF16)
        for h in range(HALVES):
            for g in range(PASSES):
                d_fours[h, g] = kept("d_fours%d%d" % (h, g), [P, HALF, PACK], BF16)
                d_codes[h, g] = kept("d_codes%d%d" % (h, g), [P, HALF], U32)
                d_plane[h, g] = kept("d_plane%d%d" % (h, g), [P, HALF], U8)
        weighted, y32, y16, y_fours = {}, {}, {}, {}
        for h in range(HALVES):
            for i in range(ROW_TILES):
                weighted[h, i] = kept("weighted%d%d" % (h, i), [P, HALF], F32)
                y32[h, i] = kept("y32_%d%d" % (h, i), [P, HALF], F32)
                y16[h, i] = kept("y16_%d%d" % (h, i), [P, HALF], BF16)
        y_codes = [kept("y_codes%d" % h, [P, T], U32) for h in range(HALVES)]
        y_planes = kept("y_planes", [P, T], U8)


        def load_x(g):
            src = x_words[g].rearrange("p n t -> p (n t)")
            nc.sync.dma_start(out=x_codes[g].bitcast(I32), in_=src.bitcast(I32))

        def load_a(tile, h, first_pass, end_pass):
            src = a_words[first_pass:end_pass].rearrange("g p n -> p g n")[:, :, 2 * HALF * h : 2 * HALF * (h + 1)]
            nc.sync.dma_start(out=tile[:].bitcast(I32), in_=src.bitcast(I32))

        def load_b(h):
            src = b_words.rearrange("g p n t -> p g (n t)")[:, :, PACK * HALF * h : PACK * HALF * (h + 1)]
            nc.sync.dma_start(out=b_codes[h][:].bitcast(I32), in_=src.bitcast(I32))

        def load_d(h, g):
            rows = d[PASS_K * g : PASS_K * (g + 1), HALF * h : HALF * (h + 1)]
            nc.sync.dma_start(out=d_rows[h, g][:], in_=rows.rearrange("(p j) w -> p j w", j=PACK))

        def load_plane(plane, scales, live_rows):
            for j in live_rows:
                rows = scales.rearrange("g (q j) n -> j q g n", j=LIVE)[j]
                nc.sync.dma_start(out=plane[j:P:QUAD].bitcast(I32), in_=rows.bitcast(I32))


        def interleave_d(copy, h, g):
            copy(out=d_fours[h, g][:], in_=d_rows[h, g][:].rearrange("p t c -> p c t"))

        def quantize_d(h, g):
            nc.vector.quantize_mx(
                out=d_codes[h, g][:].bitcast(FP8X4),
                scales=d_plane[h, g][:],
                in_=d_fours[h, g][:].rearrange("p c t -> p (c t)"),
            )


        def operand_a(h, g):
            return a_codes[h, g].bitcast(FP4X4), a_plane[h][:, g, :]

        def operand_b(h, g):
            return b_codes[h][:, g, :].bitcast(FP8X4), b_planes[LIVE * (g + 1) :, HALF * h : HALF * (h + 1)]

        def operand_d(h, g, cols=slice(0, HALF)):
            return d_codes[h, g][:, cols].bitcast(FP8X4), d_plane[h, g][:, cols]

        def one_pass(bank, operand, i, g):
            codes, plane = operand
            nc.tensor.matmul_mx(
                out=bank[:],
                lhsT=x_codes[g][:, P * i : P * (i + 1)].bitcast(FP8X4),
                lhsT_scale=x_plane[:, g, P * i : P * (i + 1)],
                rhs=codes,
                rhs_scale=plane,
                start=(g == 0),
                stop=(g == PASSES - 1),
            )

        def product(operand_of, h, i):
            bank = psum.tile([P, HALF], F32, name="bank")
            for g in range(PASSES):
                one_pass(bank, operand_of(h, g), i, g)
            return bank

        def take_exp(bank, h, i):
            nc.scalar.activation(out=weighted[h, i][:], in_=bank[:], func=ACT.Exp)

        def cross(h, i):
            take_exp(product(operand_a, h, i), h, i)

        def pos(h, i):
            bank = product(operand_b, h, i)
            nc.vector.scalar_tensor_tensor(
                out=weighted[h, i][:],
                in0=bank[:],
                scalar=r_cols[:, i : i + 1],
                in1=weighted[h, i][:],
                op0=ALU.mult,
                op1=ALU.mult,
            )

        def store_y(h, i):
            nc.sync.dma_start(out=out_0[P * i : P * (i + 1), HALF * h : HALF * (h + 1)], in_=y32[h, i][:])

        def rest(h, i):
            bank = product(operand_d, h, i)
            nc.vector.tensor_tensor(out=y32[h, i][:], in0=bank[:], in1=weighted[h, i][:], op=ALU.add)
            store_y(h, i)


        def by_pairs(ap):
            return ap.rearrange("p (q u e) -> p u q e", u=2, e=2)

        def sorted_pairs(h, i):
            return y16[h, i][:].rearrange("p (u q e) -> p u q e", u=2, e=2)

        def round_y(h, i):
            nc.scalar.copy(out=sorted_pairs(h, i), in_=by_pairs(y32[h, i][:]))

        def last_rest(h, i):
            width = HALF // 2
            parts = []
            for c in range(2):
                cols = slice(width * c, width * (c + 1))
                bank = psum.tile([P, width], F32, name="bank")
                for g in range(PASSES):
                    one_pass(bank, operand_d(h, g, cols), i, g)
                parts.append((bank, cols))
            for c, (bank, cols) in enumerate(parts):
                nc.vector.tensor_tensor(
                    out=sorted_pairs(h, i)[:, :, P // 2 * c : P // 2 * (c + 1), :],
                    in0=by_pairs(bank[:]),
                    in1=by_pairs(weighted[h, i][:, cols]),
                    op=ALU.add,
                )
            for bank, cols in parts:
                nc.vector.tensor_tensor(out=y32[h, i][:, cols], in0=bank[:], in1=weighted[h, i][:, cols], op=ALU.add)
            store_y(h, i)

        def turn(h, tiles):
            bank = psum.tile([P, 2, 2, P], F32, name="bank")
            for j, i in enumerate(tiles):
                pairs = y16[h, i][:].bitcast(F32)
                for u in range(2):
                    nc.tensor.transpose(bank[:, j, u, :], pairs[:, P * u : P * (u + 1)], ident[:])
            return bank

        def join_pairs(bank, h, tiles):
            count = len(tiles)
            y_fours[h, tiles[0]] = kept("y_fours%d%d" % (h, tiles[0]), [P, count * P * PACK], BF16)
            nc.scalar.copy(
                out=y_fours[h, tiles[0]][:].bitcast(F32).rearrange("p (j m u) -> p j m u", j=count, u=2),
                in_=bank[:, 0:count].rearrange("p j u m -> p j m u"),
            )

        def quantize_y(h, tiles):
            tracks = slice(P * tiles[0], P * (tiles[-1] + 1))
            nc.vector.quantize_mx(
                out=y_codes[h][:, tracks].bitcast(FP8X4),
                scales=y_planes[LIVE * h :, tracks],
                in_=y_fours[h, tiles[0]][:],
            )

        def store_words(h, first_tile, end_tile):
            dst = out_1[h].rearrange("p m t -> p (m t)")[:, PACK * P * first_tile : PACK * P * end_tile]
            nc.sync.dma_start(out=dst.bitcast(I32), in_=y_codes[h][:, P * first_tile : P * end_tile].bitcast(I32))

        def store_scales(queue, q):
            queue.dma_start(
                out=out_2[:, LIVE * q : LIVE * (q + 1), :].bitcast(I32),
                in_=y_planes[QUAD * q : QUAD * q + LIVE * HALVES, :].bitcast(I32),
            )

        nc.vector.memset(a_plane[0][:].bitcast(I32), 0)
        nc.vector.memset(x_plane[:].bitcast(I32), 0)
        load_a(a_first, 0, 0, 1)
        load_plane(a_plane[0], a_scales[:, :, 0:HALF], range(1))
        load_x(0)
        load_plane(a_plane[0], a_scales[:, :, 0:HALF], range(1, LIVE))
        load_plane(x_plane, x_scales, range(LIVE))

        nc.gpsimd.memset(b_planes[:].bitcast(I32), 0)
        nc.gpsimd.memset(r_rows[:], 0.0)
        for q in range(QUADS):
            nc.gpsimd.dma_start(
                out=b_planes[QUAD * q + LIVE : QUAD * q + LIVE * (PASSES + 1), :].bitcast(I32),
                in_=b_scales[:, LIVE * q : LIVE * (q + 1), :].bitcast(I32),
            )
        for q in range(QUADS):
            nc.gpsimd.dma_start(
                out=r_rows[QUAD * q : QUAD * q + ROW_TILES, :],
                in_=r.rearrange("(i q a) -> q i a", q=QUADS, a=QUAD)[q],
            )
        make_identity(nc, ident[:])

        nc.vector.memset(a_plane[1][:].bitcast(I32), 0)
        load_x(1)
        load_a(a_next, 0, 1, PASSES)
        load_x(2)
        load_a(a_high, 1, 0, PASSES)
        load_plane(a_plane[1], a_scales[:, :, HALF:N], range(LIVE))
        load_d(0, 0)
        load_d(0, 1)
        load_b(0)
        load_d(0, 2)
        load_d(1, 0)
        load_b(1)
        load_d(1, 1)
        load_d(1, 2)

        banks = [psum.tile([P, HALF], F32, name="bank") for i in range(ROW_TILES)]
        for g in range(PASSES):
            for i in range(ROW_TILES):
                one_pass(banks[i], operand_a(0, g), i, g)
        for i in range(ROW_TILES):
            take_exp(banks[i], 0, i)
        for i in range(ROW_TILES):
            cross(1, i)

        interleave_d(nc.vector.tensor_copy, 0, 0)
        quantize_d(0, 0)
        interleave_d(nc.vector.tensor_copy, 0, 1)
        nc.vector.transpose(out=r_cols[:], in_=r_rows[:])
        quantize_d(0, 1)
        interleave_d(nc.vector.tensor_copy, 0, 2)

        pos(0, 0)
        quantize_d(0, 2)
        for g in range(PASSES):
            interleave_d(nc.scalar.copy, 1, g)
        for i in range(1, ROW_TILES):
            pos(0, i)

        for step in range(PASSES):
            pos(1, step)
            quantize_d(1, step)
            for i in (2 * step, 2 * step + 1):
                rest(0, i)
                round_y(0, i)
        pos(1, 3)
        rest(1, 0)
        round_y(1, 0)
        rest(1, 1)

        twos = [[0, 1], [2, 3], [4, 5]]
        turned = [turn(0, tiles) for tiles in twos]
        join_pairs(turned[0], 0, twos[0])
        round_y(1, 1)
        join_pairs(turned[1], 0, twos[1])
        join_pairs(turned[2], 0, twos[2])
        pos(1, 4)
        quantize_y(0, twos[0])
        rest(1, 2)
        round_y(1, 2)
        quantize_y(0, twos[1])
        rest(1, 3)
        round_y(1, 3)
        quantize_y(0, twos[2])
        store_words(0, 0, ROW_TILES)
        rest(1, 4)

        turned = [turn(1, [0, 1]), turn(1, [2])]
        join_pairs(turned[0], 1, [0, 1])
        round_y(1, 4)
        join_pairs(turned[1], 1, [2])
        pos(1, 5)
        quantize_y(1, [0, 1])
        store_words(1, 0, 2)
        last_rest(1, 5)

        turned = [turn(1, [3, 4]), turn(1, [5])]
        join_pairs(turned[0], 1, [3, 4])
        join_pairs(turned[1], 1, [5])
        quantize_y(1, [2])
        quantize_y(1, [3, 4])
        store_words(1, 2, 5)
        quantize_y(1, [5])
        store_words(1, 5, ROW_TILES)
        for q in range(QUADS):
            store_scales(nc.scalar if q % 2 else nc.sync, q)
